import numpy as np, ml_dtypes
CORES = [83,85,87,115,117,119]
N = 6
BF = ml_dtypes.bfloat16
def gentries(a):
    return np.ascontiguousarray(a.reshape(8, 16, -1).transpose(0, 2, 1)).reshape(8, -1)
def gtable(e):
    e = np.asarray(e); return np.ascontiguousarray(e.reshape(8, -1, 16).transpose(0, 2, 1)).reshape(128, -1).astype(np.int32)
V, G, LN, RO, SH = 2048, 384, 64, 3, 3
DS = [1, 2, 5]
W = V + len(DS) * G
def graph(rng, share):
    s = rng.permutation(4 * V); n = int(4 * V * share); n = n + n % 2
    b = np.empty(4 * V, np.int64); b[s[:n]] = rng.integers(V, W, n); p = s[n:].reshape(2, -1)
    b[p[0]] = p[1] % V; b[p[1]] = p[0] % V
    return b
def marks(rng, size=1.0):
    return ((0.25 + 0.75 * rng.random((N, 8, 16, V))) * size).astype(np.float32)
def parts(rng):
    x = rng.integers(0, 4096, (N, 8, 16, V))
    nb = np.stack([np.stack([graph(rng, float(rng.choice(np.array([0.05, 0.15, 0.25])))) for g in range(8)]) for q in range(N)])
    z = (N, 8, RO, LN); k = rng.integers(0, 4, z); j = np.where(rng.random(z) < 0.95, (k + rng.integers(1, 4, z)) % 4, k)
    la = np.stack([rng.integers(0, V, z), j, k, rng.integers(0, 4, z), rng.integers(1, 17, z)])
    return x, marks(rng), nb, la
def pack(x, am, nb, la):
    d = {"x": np.ascontiguousarray(x.reshape(N, 128, V)).astype(np.int32), "am": np.ascontiguousarray(am.reshape(N, 128, V)).astype(BF), "nb": np.stack([gtable(t) for t in nb])}
    for i, name in enumerate(("lb", "pj", "pk", "pl", "hq")): d[name] = np.stack([gtable(t.reshape(8, -1)) for t in la[i]])
    return d
def setup_inputs(rng):
    return pack(*parts(rng))
def setup_inputs_spread(rng):
    x, am, nb, la = parts(rng)
    u = np.minimum(np.exp2(12.0 * rng.random(x.shape)).astype(np.int64) - 1, 4095); side = rng.random((N, 8, 1, V)) < 0.5
    return pack(np.where(side, 4095 - u, u), marks(rng, np.exp2(rng.integers(-1, 2, (N, 8, 1, V)).astype(np.float64))), nb, la)
def setup_inputs_ends(rng):
    x, am, nb, la = parts(rng); flip = rng.random(16) < 0.5; flip[0] = False; flip[15] = True; M = V // 8; late = np.arange(4, M - 1, 4)
    for q in range(N):
        for g in range(8):
            o = np.arange(1, V - 1); o = rng.permutation(o[o != G - 1])
            t = o[:4 * M].reshape(4, M).copy(); t[1, 0] = 0; t[1, 1] = V - 1; A, B, C, D = t
            col = rng.integers(0, 2, V); col[G - 1] = 1; cb = rng.integers(0, 2, M); cb[0] = 0; cb[1] = 1
            col[B] = cb; col[D] = cb; col[A] = 1 - cb; col[C] = 1 - cb
            col[A[late]] = cb[late]; col[D[late]] = 1 - cb[late]
            n = np.repeat(np.where(col == 0, W - 1, 0)[None], 4, 0); r = rng.random((4, V)) < 0.05; r[:, t.reshape(-1)] = False
            n = np.where(r, rng.integers(0, W, (4, V)), n)
            k = 3 * rng.integers(0, 2, M); j = 3 - k
            n[k, B] = A; n[j, B] = C; n[k, C] = D; n[j, C] = B; n[j, A] = B; n[k, D] = C
            nb[q, g] = n.reshape(-1)
            v = np.repeat(col[None], 16, 0); odd = t[:, 3:M - 1:2].reshape(-1); v[:, odd] = rng.integers(0, 2, (16, len(odd)))
            x[q, g] = 4095 * np.where(flip[:, None], 1 - v, v)
            b = np.where(rng.random((RO, LN)) < 0.7, rng.integers(0, 2, (RO, LN)), rng.integers(2, M - 1, (RO, LN))); b[:, LN - 1] = M - 1; b[:, LN - 2] = M - 4
            void = rng.random((RO, LN)) < 0.1; void[:, LN - 2:] = False
            la[0, q, g] = B[b]; la[2, q, g] = k[b]; la[3, q, g] = k[b]; la[1, q, g] = np.where(void, k[b], j[b])
    la[4] = np.where(rng.random(la[4].shape) < 0.5, 1, 16)
    am = rng.choice(np.array([0.125, 4.0], np.float32), am.shape)
    return pack(x, am, nb, la)
def tie(rng, n, t, more):
    p = np.argsort(rng.random((4, t.shape[1], 4)), axis=-1); A, B, C, D = t
    for i, names in enumerate(([B] + more[0], [A, C] + more[1], [B, D] + more[2], [C] + more[3])):
        for s, name in enumerate(names): n[p[i, :, s], t[i]] = name
    return p[1, :, 1], p[1, :, 0], p[2, :, 1]
def setup_inputs_calm(rng):
    x, am, nb, la = parts(rng); K = RO * LN; ki = np.arange(K) % 16; nl = K // 16; nk = 11 * nl; Q = 2 ** SH; late = np.arange(nl) * 16 // LN
    am = (0.125 + 0.125 * rng.random(am.shape)).astype(np.float32)
    a1 = 4 * nk; a2 = a1 + 12 * nl; a3 = a2 + 16 * nl; a4 = a3 + 6; a5 = a4 + RO * (3 * RO + 1) // 2
    for q in range(N):
        for g in range(8):
            o = rng.permutation(V); n = nb[q, g].reshape(4, V); xs = x[q, g]
            rest = o[a5:]; few = rest[rest >= G][:64]; fa, fb, fc, fd = few.reshape(4, 16)
            n[np.isin(n, fb)] = o[a3]
            own = np.concatenate([o[:a5], few]); n[:, own] = own
            L = np.zeros((5, K), np.int64)
            t = o[:a1].reshape(4, nk); A, B, C, D = t; m = ki < 11
            L[1, m], L[2, m], L[3, m] = tie(rng, n, t, [[A] * 3, [B] * 2, [C] * 2, [D] * 3])
            v = rng.choice(np.array([0, 1, 2, 3, 8, 15, 16]), nk); up = np.argsort(rng.random((16, nk)), axis=0) < v
            base = rng.integers(0, 2048, (16, nk)); flat = rng.integers(0, 4096, (16, nk))
            for i, step in enumerate((0, 1024, 2048, 2048)): xs[:, t[i]] = np.where(up, base + step, flat)
            L[0, m] = B; L[4, m] = np.clip(v + rng.integers(0, 2, nk), 1, 16)
            c = o[a1:a2].reshape(2, 6, nl); m = ki == 15
            for h in range(2):
                for i in range(6):
                    n[0, c[h, i]] = c[h, max(i - 1, 0)]; n[3, c[h, i]] = c[h, min(i + 1, 5)]; xs[:, c[h, i]] = 819 * i
            n[1, c[0, 2]] = c[1, 2]; n[2, c[1, 2]] = c[0, 2]
            L[0, m] = c[0, 2]; L[1, m] = 1; L[4, m] = 1
            p = rng.integers(2, 2049, 16); far = rng.integers(p + 2047, 4096)
            va = int(rng.choice(np.array([1, 2, 3, 8, 15, 16]))); act = (np.argsort(rng.random(16)) < va).astype(np.int64)
            xs[:, o[a3:a4]] = np.stack([p, p - 1, p + 1, p - 2, far - 1, p + 1025], axis=1)
            h0, hm, hp, h2, hc, one = [int(u) for u in o[a3:a4]]
            z = a4; tip = np.zeros(RO, np.int64)
            for r in range(RO):
                s = o[z:z + 3 * r + 2]; z += 3 * r + 2
                for i in range(3 * r + 2): xs[:, s[i]] = p + 1024 * (1 - i % 2) + i * (Q - 1)
                xs[:, s[-1]] = xs[:, s[-1]] + act
                n[0, s[:-1]] = s[1:]; tip[r] = s[0]
            for e in range(4):
                t = o[a2 + 4 * nl * e:a2 + 4 * nl * (e + 1)].reshape(4, nl); A, B, C, D = t; m = ki == 11 + e
                if e in (0, 3):
                    for i, at in enumerate((p, p - 1, far, p)): xs[:, t[i]] = at[:, None]
                    more = [[hm, hp, hp], [h2, h0], [hc, hc], [hm, hp, hp]]
                    if e == 3: more[0] = [hp, tip[late], one]
                else:
                    for i in range(4): xs[:, t[i]] = p[:, None]
                    more = [[A] * 3, [B] * 2, [C] * 2, [D] * 3]; w = rng.integers(1, 4, nl)
                    if e == 1: more[0] = [one, np.where(w > 1, one, A), np.where(w > 2, one, A)]
                    if e == 2: more[0] = [tip[late], A, A]
                L[1, m], L[2, m], L[3, m] = tie(rng, n, t, more); L[0, m] = B
                L[4, m] = rng.integers(1, 17, nl) if e < 2 else np.minimum(va + np.arange(nl) % 2, 16)
            d = 1024 + np.where(rng.random((16, 16)) < 0.5, -1, 1) * rng.integers(900, 1017, (16, 16)); mid = rng.integers(d, 4096 - d); side = np.where(rng.random((16, 16)) < 0.5, -1, 1)
            xs[:, fa] = mid; xs[:, fb] = mid + side * d; xs[:, fc] = mid - side * d; xs[:, fd] = mid + side * d
            n[0, fa] = fb; n[1, fa] = fc; n[2, fa] = fb; n[3, fa] = fc; n[:, fb] = fd
            am[q, g][:, fb] = 4.0
            la[:, q, g] = L.reshape(5, RO, LN)
    return pack(x, am, nb, la)
def setup_inputs_corners(rng):
    x, am, nb, la = parts(rng)
    am = np.where(rng.random(am.shape) < 0.06, 0.125, np.exp2(-3.0 + 2.0 * rng.random(am.shape))).astype(np.float32)
    x = np.where(rng.random(x.shape) < 0.8, rng.choice(np.array([0, 1, 1023, 1024, 1025, 2047, 2048, 4094, 4095]), x.shape), x)
    for q in range(N):
        for g in range(8):
            n = nb[q, g].reshape(4, V); ty = (g + q) % 6
            if ty == 0: n[:] = rng.integers(V, W, (4, V))
            if ty == 1:
                for k in (0, 1, 3):
                    m = rng.permutation(V).reshape(2, -1); n[k, m[0]] = m[1]; n[k, m[1]] = m[0]
                n[2] = n[0]
            if ty == 2:
                m = rng.permutation(V)[:5 * (V // 10)].reshape(5, -1)
                for i in range(5):
                    for k in range(4): n[k, m[i]] = m[(i + 1 + k) % 5]
            if ty == 3: n[:] = rng.integers(0, V, (4, V))
            if ty == 4: n[:] = np.where(rng.random((4, V)) < 0.1, np.arange(V)[None], n)
            if ty == 5: n[:] = np.where(rng.random((4, V)) < 0.3, rng.choice(np.array([0, V - 1, V, W - 1]), (4, V)), n)
    la[0] = np.where(rng.random(la[0].shape) < 0.1, rng.choice(np.array([0, V - 1]), la[0].shape), la[0])
    la[4] = rng.choice(np.array([1, 2, 15, 16]), la[4].shape)
    return pack(x, am, nb, la)
def block(n, a, b, c, d):
    n[0, b] = a; n[3, b] = c; n[2, c] = b; n[0, c] = d; n[1, a] = b; n[2, d] = c
def setup_inputs_crowd(rng):
    x, am, nb, la = parts(rng)
    for q in range(N):
        for g in range(8):
            n = nb[q, g].reshape(4, V); ty = (g + q) % 5; o = rng.permutation(V); L = la[:, q, g]; z = int(rng.integers(0, 4))
            if ty <= 1:
                at = o[:2 * LN + 9]; n[:, at] = rng.integers(V, W, (4, len(at)))
                h = o[0]; D = o[1:5]; B = o[5:5 + LN]; A = o[5 + LN:5 + 2 * LN]
                n[:, h] = D; n[0, D] = h; n[0, B] = A; n[3, B] = h; n[1, A] = B
                for t in range(RO): L[0, t] = rng.permutation(B)
                L[1] = 3; L[2] = 0; L[1, 0, :z] = 0
                if ty == 1:
                    a, b, c, d = o[5 + 2 * LN:9 + 2 * LN]; block(n, a, b, c, d); L[0, :, LN - 1] = b; L[3, :, LN - 1] = 0
            if ty == 2:
                n[:, o[:4]] = rng.integers(V, W, (4, 4)); block(n, o[0], o[1], o[2], o[3])
                L[0] = o[1]; L[1] = 3; L[2] = 0; L[3] = 0; L[1, :, :z] = 0
            if ty == 3:
                m = o[:3 * LN + 1]; n[:, m] = rng.integers(V, W, (4, len(m))); n[0, m[1:]] = m[:-1]; n[3, m[:-1]] = m[1:]
                for t in range(RO): L[0, t] = m[3 * (np.arange(LN) if t == 0 else rng.permutation(LN)) + 1]
                L[1] = 3; L[2] = 0; L[3] = 3
            if ty == 4:
                e = int(rng.integers(1, RO)); L[1, e] = L[2, e]; L[4, e - 1, ::2] = 1
    return pack(x, am, nb, la)
def check_ranges(d):
    bad = []
    for k, lo, hi in (("x", 0, 4095), ("nb", 0, W - 1), ("lb", 0, V - 1), ("pj", 0, 3), ("pk", 0, 3), ("pl", 0, 3), ("hq", 1, 16)):
        if np.min(d[k]) < lo or np.max(d[k]) > hi: bad.append("range of " + k)
    m = np.asarray(d["am"]).astype(np.float32)
    if not np.all((m >= 0.125) & (m <= 4.0)): bad.append("range of am")
    return bad
def full(s, r):
    return np.concatenate([s[r]] + [np.roll(s[(r - DS[b]) % N], -b, axis=0)[..., :G] for b in range(len(DS))], axis=2)
def pick(w, n):
    return np.stack([w[g][:, n[g].reshape(-1)] for g in range(8)]).reshape(8, 16, 4, V)
def pulls(w, n):
    d = pick(w, n) - w[:, :, None, :V]
    return np.clip(d - 1024 * np.sign(d), -1023, 1023)
def sweep(s, n, stress):
    new, e = [], []
    for r in range(N):
        p = pulls(full(s, r), n[r])
        if stress: e.append(np.sum(p * p, axis=2))
        new.append(np.clip(s[r] + (np.sum(p, axis=2) >> SH), 0, 4095).astype(np.int32))
    return np.stack(new), e
def winners(n, B, j, k, l):
    A = n[k, B]; C = n[j, B]; c = np.minimum(C, V - 1); D = n[l, c]; a = np.minimum(A, V - 1); d = np.minimum(D, V - 1)
    pa = n[:, a] == B; pd = n[:, d] == C
    good = (A < V) & (C < V) & (D < V) & (A != B) & (A != C) & (A != D) & (B != C) & (B != D) & (C != D)
    good = good & np.any(pa, axis=0) & np.any(pd, axis=0) & ~np.any(n[:, a] == C, axis=0) & ~np.any(n[:, d] == B, axis=0)
    who = np.stack([A, B, C, D]); i = np.arange(LN); first = np.full(W, LN)
    np.minimum.at(first, who[:, good], np.broadcast_to(i, (4, LN))[:, good])
    w = np.nonzero(good & np.all(first[who] >= i, axis=0))[0]
    port = np.stack([np.argmax(pa, axis=0), k, l, np.argmax(pd, axis=0)])
    return w, who[:, w], (port * V + who)[:, w], np.stack([C, D, A, B])[:, w]
def reference(x, am, nb, lb, pj, pk, pl, hq):
    s = x.astype(np.int32).reshape(N, 8, 16, V)
    n = np.stack([gentries(t) for t in nb]).astype(np.int64).reshape(N, 8, 4, V)
    la = [np.stack([gentries(t) for t in u]).astype(np.int64).reshape(N, 8, RO, LN) for u in (lb, pj, pk, pl, hq)]
    for t in range(RO):
        s, e1 = sweep(s, n, True)
        done = []
        for r in range(N):
            for g in range(8):
                w, who, at, name = winners(n[r, g], la[0][r, g, t], la[1][r, g, t], la[2][r, g, t], la[3][r, g, t])
                flat = n[r, g].reshape(-1); old = flat[at]; flat[at] = name; done.append((r, g, w, who, at, old))
        s, e2 = sweep(s, n, False)
        s, e3 = sweep(s, n, True)
        for r, g, w, who, at, old in done:
            worse = np.sum(e3[r][g][:, who], axis=1) > np.sum(e1[r][g][:, who], axis=1)
            back = np.sum(worse, axis=0) >= la[4][r, g, t, w]
            flat = n[r, g].reshape(-1); flat[at[:, back]] = old[:, back]
    m = am.astype(np.float32).astype(np.float64).reshape(N, 8, 16, V); y = []
    for r in range(N):
        p = pulls(full(s, r), n[r]).astype(np.float64)
        y.append(np.sum(pick(full(m, r), n[r]) * np.exp(p * p * (-2.0 ** -19)), axis=2).reshape(128, V))
    return {"y": np.stack(y).astype(np.float32)}

def check_inputs(d):
    bad = list(check_ranges(d))
    if not bad:
        for name, y in reference(**d).items():
            for q in range(N):
                v = np.abs(np.asarray(y[q], np.float64)); s = np.sqrt(np.mean(v * v))
                if v.max() > 5 * s or s < 2.0 ** -2: bad.append('%s of rank %d is uneven or too small' % (name, q))
    return bad

from concourse.bass import DstId, RemoteDMATransfer
from concourse.mybir import AluOpType as OP, ActivationFunctionType as AF

V, GH, NW, RO = 2048, 384, 3200, 3
DS = [1, 2, 5]
M = 12582912.0
RW, TRASH = 2432, 2176
CHUNKS = [[[384, 512, 512, 384, 256], ['pPbB', 'aabb', 'vpaA', 'pabB', 'vAAA']], [[384, 512, 512, 384, 256], ['vvpb', 'vPAb', 'vvVa', 'vvPA', 'VpBB']],
          [[384, 512, 512, 384, 256], ['vVAB', 'vvbb', 'VVPa', 'vpaB', 'vppb']], [[256, 512, 512, 512, 256], ['PABB', 'vvAB', 'vPbB', 'vvVV', 'vvVa']]]
ALAT, ACOST = 2.4, 1.0
WAIT, PASSES, NS = 0.0, 1, 4
GCP = True
WI = True
GC, CY, PEC, LAT, DLAT, RLAT = 1.56, 0.00083, 0.00042, 0.12, 2.2, 3.5

F32, F16, BF, I32, U16 = "float32", "float16", "bfloat16", "int32", "uint16"
SB = {"C16": (8192, F16), "S16": (8192, F16), "J8": (128, F16), "JS": (128, F16), "OWN": (V, F16), "R4": (RW, F32), "MW": (NW, BF),
      "XS": (V, I32), "XR": (768, I32), "SND": (768, F32), "MS": (768, BF), "NBI": (512, I32), "W32": (512, F32),
      "WA": (512, U16), "WB": (512, U16), "J": (256, I32), "JT": (256, I32), "QA": (4, I32), "QI": (8, I32), "QF": (8, F32),
      "QAF": (4, F32), "I1": (128, F16), "I8": (128, F16), "IS": (128, F16), "IM": (128, F16), "IK": (128, F16), "IF": (128, F32),
      "ONE": (512, BF), "CM": (128, BF), "CN": (128, BF), "CO": (128, BF), "BLK": (128, F16), "B0H": (128, F16), "B0N": (128, F16),
      "B0F": (128, F32), "LOW": (128, F16), "LT0": (128, F16), "TA": (512, F32), "DG": (192, F32), "TRI": (256, F16),
      "SEG": (1024, BF), "SG4": (256, BF), "TR": (16, F32), "REP": (60, U16), "LT": (64, I32), "EX": (960, F16),
      "LBF": (12, F32), "KPB": (12, F32), "KB": (12, U16), "MK": (192, F32), "MJ": (192, F32), "ML": (192, F32),
      "QR": (192, F32), "XB": (192, F32), "X": (256, F32), "XL": (256, F16), "ROWS": (256, F32), "NEW": (256, F32),
      "MM": (192, F32), "WR": (320, F32), "SC": (320, F32), "H": (16, I32), "TT": (16, F32), "KP": (16, F32), "OF": (16, U16),
      "FL": (640, F16), "FI": (128, F16), "GOOD": (64, F32), "WIN": (64, F32), "Y": (640, F16), "E": (3072, F16),
      "S4": (256, F32), "KD": (16, F32), "KO": (16, F32), "OS": (16, U16), "DL": (256, F32), "DV": (256, F32),
      "SL": (128, U16), "AL": (16, U16), "O16": (256, F16),
      "E1": (64, F32), "WO": (64, F16), "KEEP": (64, F32)}
NP = 6
for _n in range(NP):
    SB["P%d" % _n] = (NW, I32 if WI else F32)
SB["FZ"] = (8192, F32)
if WI: del SB["SND"], SB["CM"], SB["CN"]
SCRATCH = {k: ("sbuf", [128, v[0]], v[1]) for k, v in SB.items()}
SCRATCH["OWN"] = ("sbuf", [128, 4, V], F16)
PS = ["S0", "S1", "S2", "D0", "D1", "D2", "L0", "L1"]
for _n in PS:
    SCRATCH[_n] = ("psum", [128, 512], F32)
for _n in range(1, 10):
    SCRATCH["G%d" % _n] = ("dram", [160, GH], I32 if WI else F32)
NDMA = 130
SEMAPHORES = ["cv", "ca", "cp", "cg", "sent", "arrm"] + ["arr%d" % n for n in range(10)] + ["dm%d" % n for n in range(NDMA)]


def A(name, lo=0, hi=None, step=1):
    return ("ap", name, lo, (SB[name][0] if name in SB else 512) if hi is None else hi, step)


def IND(win, off):
    return ("ind", win, off)


def _n(s):
    return 16 * _n(s[2]) if s[0] == "ind" else len(range(s[2], s[3], s[4]))


def _ap(T, s):
    if not isinstance(s, tuple):
        return s
    if s[0] == "ind":
        return _ap(T, s[1]).indirect(_ap(T, s[2]))
    if s[1] == "OWN":
        return T.OWN[:, 0, s[2]:s[3]]
    return T[s[1]][:, s[2]:s[3]] if s[4] == 1 else T[s[1]][:, s[2]:s[3]:s[4]]


def kinds(L):
    return "".join(sorted(L, key=lambda c: "vVpPaAbB".index(c)))


def runs(L):
    cut = [i for i in range(len(L)) if i == 0 or L[i] != L[i - 1]] + [len(L)]
    return list(zip(cut, cut[1:]))


def _two(s):
    return s[0] == "ap" and s[1] in SB and SB[s[1]][1] in (F16, BF, U16)


def build():
    ops, rec = [], {}

    def add(eng, fn, reads, writes, cost, lat=LAT, extra=()):
        k = len(ops); deps = set(extra); rd, wr = [], []
        for s in reads:
            if isinstance(s, tuple):
                rd += [s[1], s[2]] if s[0] == "ind" else [s]
        for s in writes:
            if s[0] == "ind":
                wr.append(s[1]); rd.append(s[2])
            else:
                wr.append(s)
        acc = [(s, False) for s in rd] + [(s, True) for s in wr]
        acc = [((s[1], 0, 512, True) if s[1] in PS else (s[1], s[2], s[3], w)) for s, w in acc]
        for nm, lo, hi, w in acc:
            for (a, b, o, ow) in rec.get(nm, []):
                if a < hi and lo < b and (w or ow):
                    deps.add(o)
        for (s, w0), (nm, lo, hi, w) in zip([(s, False) for s in rd] + [(s, True) for s in wr], acc):
            L = rec.setdefault(nm, [])
            if w and (nm in PS or s[4] == 1):
                L[:] = [r for r in L if not (lo <= r[0] and r[1] <= hi)]
            L.append((lo, hi, k, w))
        deps.discard(k)
        ops.append({"eng": eng, "fn": fn, "deps": sorted(deps), "cost": cost, "lat": lat, "lab": wr[0][1:3] if wr else "",
                    "gn": sum(_n(s) for s in reads if isinstance(s, tuple) and s[0] == "ind")})
        return k

    def vc(out, ins, tt=False):
        n = _n(out)
        if out[0] == "ind": return 0.05 + n * 3.5 * CY
        if ins[0][0] == "ind": return 0.05 + n * GC * CY
        c = 0.5 if all(_two(s) for s in [out] + ins) else 1.0
        if tt and all(s[1] not in PS for s in ins): c *= 2
        return 0.03 + max(64, n * c) * CY

    def ts(out, a, s1, op0, s2=None, op1=None):
        if op1 is None:
            fn = lambda g, T, c: g.vector.tensor_scalar(_ap(T, out), _ap(T, a), _ap(T, s1), None, op0)
        else:
            fn = lambda g, T, c: g.vector.tensor_scalar(_ap(T, out), _ap(T, a), _ap(T, s1), _ap(T, s2), op0, op1)
        return add("v", fn, [a, s1, s2], [out], vc(out, [a]))

    def tt(out, a, b, op):
        return add("v", lambda g, T, c: g.vector.tensor_tensor(_ap(T, out), _ap(T, a), _ap(T, b), op), [a, b], [out], vc(out, [a, b], True))

    def cp(out, a):
        return add("v", lambda g, T, c: g.vector.tensor_copy(_ap(T, out), _ap(T, a)), [a], [out], vc(out, [a]))

    def scan(out, seg, a):
        return add("v", lambda g, T, c: g.vector.tensor_tensor_scan(_ap(T, out), _ap(T, seg), _ap(T, a), 0.0, OP.mult, OP.add),
                   [seg, a], [out], vc(out, [seg, a]))

    def ms(out, val):
        return add("v", lambda g, T, c: g.vector.memset(_ap(T, out), val), [], [out], vc(out, [out]))

    def act(out, a, func, bias=0.0, scale=1.0):
        n = _n(out)
        cost = 0.065 + n * GC * CY if a[0] == "ind" else 0.05 + max(64, n) * CY
        return add("a", lambda g, T, c: g.scalar.activation(_ap(T, out), _ap(T, a), func, bias=bias, scale=scale), [a], [out], cost)

    def mm(out, l, r, start, stop):
        cost = max(64, _n(r)) * PEC * (4 if SB[r[1]][1] == F32 else 1) + 0.01
        return add("p", lambda g, T, c: g.tensor.matmul(_ap(T, out), _ap(T, l), _ap(T, r), start, stop), [l, r], [out], cost)

    def dma(pairs, reads, writes, eng="s", lat=DLAT):
        k = add(eng, pairs, reads, writes, 0.06 * len(pairs), lat)
        ops[k]["dma"] = True
        return k

    arrived = []

    def send(srcs, dst, sem, reads, after=()):
        k = add("g", ("send", srcs, dst, sem), reads, [], 0.8, RLAT, extra=after)
        arrived.append(add("x", sem, [], [A(dst, V, NW)], 0.0, LAT, extra=[k]))

    def iota(out, pat, cm):
        return add("g", lambda g, T, c: g.iota(_ap(T, out), pat, 0, cm), [], [out], 0.13 + 2 * _n(out) * CY)

    def gcp(out, a):
        if not GCP: return act(out, a, AF.Identity)
        n = _n(out)
        return add("g", lambda g, T, c: g.affine_select(_ap(T, out), _ap(T, a), [[0, n]], OP.is_ge, 0.0, 0, 0), [a], [out], 0.17 + 2 * n * CY)

    def rolled(src, dst):
        return [lambda T, b=b, h=h: ((T[dst][0:128 - 16 * b, (b - 1) * GH:b * GH], T[src][16 * b:128, 0:GH]) if h == 0 else
                                     (T[dst][128 - 16 * b:128, (b - 1) * GH:b * GH], T[src][0:16 * b, 0:GH])) for b in (1, 2) for h in (0, 1)]

    if WI:
        dma([lambda T: (T.P0[:, 0:GH], T.x[:, 0:GH])] + rolled("x", "XR")[0:2], [], [A("P0", 0, GH), A("XR", 0, GH)])
        dma(rolled("x", "XR")[2:4], [], [A("XR", GH, 768)], eng="a")
        send([lambda T: T.P0[:, 0:GH], lambda T: T.XR[:, 0:GH], lambda T: T.XR[:, GH:768]], "P0", "arr0", [A("P0", 0, GH), A("XR")])
        dma([lambda T: (T.NBI[:], T.nb[:])], [], [A("NBI")], eng="a")
        dma([lambda T: (T.XS[:], T.x[:])], [], [A("XS")], lat=3.5)
        dma([lambda T: (T.P0[:, GH:V], T.x[:, GH:V])], [], [A("P0", GH, V)], lat=4.5)
        act(A("OWN"), A("XS"), AF.Identity, bias=-2048.0)
        act(A("W32"), A("NBI"), AF.Identity)
    else:
        dma([lambda T: (T.XS[:, 0:GH], T.x[:, 0:GH])] + rolled("x", "XR")[0:2], [], [A("XS", 0, GH), A("XR", 0, GH)])
        dma(rolled("x", "XR")[2:4], [], [A("XR", GH, 768)], eng="a")
        dma([lambda T: (T.XS[:, GH:V], T.x[:, GH:V])], [], [A("XS", GH, V)], lat=3.5)
        dma([lambda T: (T.NBI[:], T.nb[:])], [], [A("NBI")], eng="a")
        ts(A("P0", 0, GH), A("XS", 0, GH), -2048.0, OP.add)
        ts(A("SND"), A("XR"), -2048.0, OP.add)
        send([lambda T: T.P0[:, 0:GH], lambda T: T.SND[:, 0:GH], lambda T: T.SND[:, GH:768]], "P0", "arr0", [A("P0", 0, GH), A("SND")])
        ts(A("P0", GH, V), A("XS", GH, V), -2048.0, OP.add)
        act(A("OWN"), A("P0", 0, V), AF.Identity)
        cp(A("W32"), A("NBI"))
    cp(A("WA"), A("NBI"))
    dma([lambda T, i=i, n=n: (T.LT[:, 12 * i:12 * i + 12], T[n][:]) for i, n in enumerate(("lb", "pj", "pk", "pl", "hq"))], [], [A("LT")])
    ms(A("ONE"), 1.0); ms(A("CO"), -0.4375 / 128)
    for i in range(5):
        act(A("R4", 512 * i, min(RW, 512 * i + 512)), A("ONE", 0, min(512, RW - 512 * i)), AF.Identity, scale=0.0)
    dma([lambda T, p=p: (T.R4[4 * p:128:16, 0:V], T.W32[:, 128 * p:128 * p + 128]) for p in range(4)], [A("W32")], [A("R4", 0, V)])
    dma([lambda T: (T.MW[:, 0:V], T.am[:])] + rolled("am", "MS"), [], [A("MW", 0, V), A("MS")])

    iota(A("J"), [[1, 256]], 0); iota(A("QA"), [[1, 4]], 1)
    q = A("QA", 0, 1)
    ts(A("QI", 0, 1), q, 4, OP.arith_shift_right); ts(A("QI", 1, 2), q, 2, OP.arith_shift_right)
    ts(A("QI", 2, 3), q, 15, OP.bitwise_and); ts(A("QI", 3, 4), q, 3, OP.bitwise_and)
    ts(A("QI", 4, 5), q, 2, OP.arith_shift_right, 3, OP.bitwise_and)
    cp(A("QF", 0, 5), A("QI", 0, 5)); cp(A("QAF"), A("QA"))
    gq, hq, sq, pq, a0, qf = A("QF", 0, 1), A("QF", 1, 2), A("QF", 2, 3), A("QF", 4, 5), A("QF", 5, 6), A("QAF", 0, 1)
    ts(a0, A("QF", 3, 4), 0.0, OP.is_equal)
    ts(A("QF", 6, 7), sq, 1.0 / 128, OP.mult, TRASH / 128.0, OP.add)
    j = A("J", 0, 128)
    ts(A("IF"), j, qf, OP.is_equal)
    for nm, val in (("I1", 1.0), ("I8", 0.125), ("IS", -128.0), ("J8", -0.125), ("JS", 128.0), ("IM", -1.0), ("IK", -1024.0)):
        act(A(nm), A("IF"), AF.Identity, scale=val)
    if not WI:
        ms(A("CM"), M / 128); ms(A("CN"), -M / 128)
    ts(A("JT", 0, 128), j, 4, OP.arith_shift_right)
    ts(A("BLK"), A("JT", 0, 128), gq, OP.is_equal)
    ts(A("B0F"), A("JT", 0, 128), gq, OP.is_equal, a0, OP.mult)
    act(A("B0H"), A("B0F"), AF.Identity); act(A("B0N"), A("B0F"), AF.Identity, scale=-1.0)
    ts(A("JT"), A("J"), 2, OP.arith_shift_right)
    ts(A("LT0"), A("JT", 0, 128), hq, OP.is_gt, a0, OP.mult)
    tt(A("LOW"), A("LT0"), A("BLK"), OP.mult)
    ts(A("TRI"), A("JT"), sq, OP.is_le, 10000.0, OP.mult)
    ts(A("JT", 0, 192), A("J", 0, 192), 15, OP.bitwise_and)
    ts(A("DG"), A("JT", 0, 192), sq, OP.is_equal)
    for a in range(4):
        ts(A("TA", 128 * a, 128 * a + 128), j, A("QAF", a, a + 1), OP.is_equal, a0, OP.mult)
    ms(A("SEG"), 1.0); ms(A("SEG", 0, 1024, 16), 0.0); ms(A("SG4"), 1.0); ms(A("SG4", 0, 256, 4), 0.0)
    ts(A("TR"), A("J", 0, 16), 0.125, OP.mult, A("QF", 6, 7), OP.add)
    cp(A("REP"), A("J", 0, 60))

    def kappa(v, lo, hi, kp, off):
        ts(A("H", lo, hi), v, 1.0 / 16, OP.mult, -7.5 / 16, OP.add)
        ts(A("TT", lo, hi), A("H", lo, hi), -2047.0 / 128, OP.mult)
        tt(kp, A("TT", lo, hi), v, OP.add)
        ts(off, kp, 128.0, OP.mult)

    for i in range(5):
        tt(A("EX", 192 * i, 192 * i + 192), IND(A("LT", 0, 60), A("REP", 12 * i, 12 * i + 12)), A("DG"), OP.mult)
    mm(A("L0", 0, 384), A("BLK"), A("EX", 0, 384), True, True)
    mm(A("L1", 0, 384), A("BLK"), A("EX", 384, 768), True, True)
    act(A("XB"), A("L0", 0, 192), AF.Identity)
    ts(A("MJ"), A("L0", 192, 384), pq, OP.is_equal)
    ts(A("MK"), A("L1", 0, 192), pq, OP.is_equal)
    ts(A("ML"), A("L1", 192, 384), pq, OP.is_equal)
    mm(A("L0", 0, 192), A("BLK"), A("EX", 768, 960), True, True)
    act(A("QR"), A("L0", 0, 192), AF.Identity)
    cp(A("LBF"), A("LT", 0, 12))
    kappa(A("LBF"), 0, 12, A("KPB"), A("KB"))

    cnt = {"s": 0, "d": 0, "h": 0}

    def features(n, wl, cfg, k):
        raw = WI and n == 0; w = cfg[0][k]; a = sum(cfg[0][:k]); b = a + w; win = A("P%d" % (n % NP))
        L = kinds(cfg[1][k])
        C = lambda nm, p, q: A(nm, 4 * a + p * w, 4 * a + q * w)
        for p, q in runs(L.lower()):
            for i in range(p, q):
                gat = IND(win, A(wl, 128 * i + a // 16, 128 * i + b // 16)); c = C("C16", i, i + 1)
                if L[i] in "vV":
                    tt(c, gat, A("XS" if raw else "OWN", a, b), OP.subtract)
                elif L[i] in "pP":
                    act(c, gat, AF.Identity, bias=-2048.0 if raw else 0.0)
                    src = A(PS[NS + cnt["d"] % (6 - NS)], 0, w); cnt["d"] += 1
                    mm(src, A("IM"), A("OWN", a, b), True, False)
                    mm(src, A("I1"), c, False, True)
                    ts(c, src, -2047.0, OP.max, 2047.0, OP.min)
                else:
                    act(c, gat, AF.Identity, bias=2048.0 if raw else 0.0, scale=-1.0)
            c = C("C16", p, q)
            if L[p] in "aAbB":
                rd = [A("OWN", a, b), c] + ([("ap", "OWR", a, b, 1)] if q - p > 1 else [])
                kk = dma([lambda T, c=c, r=q - p: (_ap(T, c), T.OWN[:, 0:r, a:b])], rd, [c], eng="g", lat=ALAT + (q - p) * w * 0.0008)
                ops[kk]["cost"] = ACOST; ops[kk]["acc"] = True
            if L[p] not in "pP":
                ts(c, c, -2047.0, OP.max, 2047.0, OP.min)
        for p, q in runs(L):
            if L[p].isupper():
                ts(C("S16", p, q), C("C16", p, q), -1.0, OP.max, 1.0, OP.min)
            else:
                act(C("S16", p, q), C("C16", p, q), AF.Sign)
        return [c in "aAbB" for c in L]

    def copies(cfg, a, b):
        r, c0 = 1, 0
        for w, L in zip(*cfg):
            L = kinds(L).lower()
            if c0 < b and a < c0 + w: r = max([r] + [q - p for p, q in runs(L) if L[p] in "ab"])
            c0 += w
        if r > 1:
            dma([lambda T, i=i: (T.OWN[:, i, a:b], T.OWN[:, 0, a:b]) for i in range(1, r)], [A("OWN", a, b)], [("ap", "OWR", a, b, 1)])

    def sweep(n, wl):
        c0 = 0; cfg = CHUNKS[n % 3]
        for k, w in enumerate(cfg[0]):
            neg = features(n, wl, cfg, k)
            b = A(PS[cnt["s"] % NS], 0, w); cnt["s"] += 1
            mm(b, A("CO"), A("ONE", 0, w), True, False)
            mm(b, A("I1"), A("OWN", c0, c0 + w), False, False)
            for p in range(4):
                mm(b, A("J8" if neg[p] else "I8"), A("C16", 4 * c0 + p * w, 4 * c0 + p * w + w), False, False)
            if not WI:
                mm(b, A("CM"), A("ONE", 0, w), False, False)
                mm(b, A("CN"), A("ONE", 0, w), False, False)
            for p in range(4):
                mm(b, A("JS" if neg[p] else "IS"), A("S16", 4 * c0 + p * w, 4 * c0 + p * w + w), False, p == 3)
            nx = "P%d" % ((n + 1) % NP)
            ts(A(nx, c0, c0 + w), b, -2048.0, OP.max, 2047.0, OP.min)
            gcp(A("OWN", c0, c0 + w), A(nx, c0, c0 + w))
            copies(CHUNKS[3 if n == 8 else (n + 1) % 3], c0, c0 + w)
            if c0 <= GH - 1 < c0 + w:
                gn = "G%d" % (n + 1)
                dma([lambda T, gn=gn, nx=nx: (T[gn][0:128, :], T[nx][:, 0:GH]), lambda T, gn=gn, nx=nx: (T[gn][128:160, :], T[nx][0:32, 0:GH])],
                    [A(nx, 0, GH)], [("ap", gn, 0, GH, 1)])
                send([lambda T, nx=nx: T[nx][:, 0:GH], lambda T, gn=gn: T[gn][16:144, :], lambda T, gn=gn: T[gn][32:160, :]],
                     nx, "arr%d" % (n + 1), [A(nx, 0, GH), ("ap", gn, 0, GH, 1)])
            c0 += w

    def relist(wl):
        dma([lambda T, p=p: (T.W32[:, 128 * p:128 * p + 128], T.R4[4 * p:128:16, 0:V]) for p in range(4)], [A("R4", 0, V)], [A("W32")], lat=2.8)
        cp(A(wl), A("W32"))

    def wrap(lo, hi, src):
        tt(A("WR", lo, hi), src, A("DG", 0, hi - lo), OP.mult)
        scan(A("SC", lo, hi), A("SEG", 0, hi - lo), A("WR", lo, hi))

    def lanes(t):
        r4 = A("R4"); l = lambda nm: A(nm, 64 * t, 64 * t + 64)
        X = lambda m: A("X", 64 * m, 64 * m + 64); R = lambda m: A("ROWS", 64 * m, 64 * m + 64)
        oB = A("KB", 4 * t, 4 * t + 4)
        gcp(X(3), l("XB")); gcp(A("XL", 3, 256, 4), l("XB"))
        tt(A("MM", 0, 64), IND(r4, oB), l("MK"), OP.mult); tt(A("MM", 64, 128), IND(r4, oB), l("MJ"), OP.mult)
        act(R(3), IND(r4, oB), AF.Identity)
        mm(A("L0", 0, 128), A("B0F"), A("MM", 0, 128), True, True)
        wrap(0, 128, A("L0", 0, 128))
        act(A("X", 0, 128), A("L0", 0, 128), AF.Identity)
        kappa(A("SC", 15, 128, 16), 0, 8, A("KP", 0, 8), A("OF", 0, 8))
        tt(A("MM", 128, 192), IND(r4, A("OF", 4, 8)), l("ML"), OP.mult)
        act(A("ROWS", 0, 128), IND(r4, A("OF", 0, 8)), AF.Identity)
        mm(A("L1", 0, 64), A("B0F"), A("MM", 128, 192), True, True)
        wrap(128, 192, A("L1", 0, 64))
        act(X(2), A("L1", 0, 64), AF.Identity)
        kappa(A("SC", 143, 192, 16), 8, 12, A("KP", 8, 12), A("OF", 8, 12))
        act(R(2), IND(r4, A("OF", 8, 12)), AF.Identity)
        for m in range(3):
            gcp(A("XL", m, 256, 4), X(m))
        F = lambda i: A("FL", 64 * i, 64 * i + 64)
        tt(F(0), R(0), X(3), OP.is_equal); tt(F(1), R(2), X(1), OP.is_equal)
        tt(F(2), R(0), X(1), OP.is_equal); tt(F(3), R(2), X(3), OP.is_equal)
        tt(A("FL", 256, 448), A("X", 0, 192), A("X", 64, 256), OP.is_equal)
        ts(A("FL", 448, 640), A("X", 0, 192), float(V), OP.is_ge)
        mm(A("L0", 0, 128), A("LOW"), A("FL", 0, 128), True, True)
        tt(A("FI"), A("FL", 0, 128), A("L0", 0, 128), OP.is_gt)
        for i in range(2, 10):
            mm(A("L1", 0, 64), A("B0N"), F(i), i == 2, False)
        mm(A("L1", 0, 64), A("B0H"), A("FI", 0, 64), False, False)
        mm(A("L1", 0, 64), A("B0H"), A("FI", 64, 128), False, True)
        ts(A("GOOD"), A("L1", 0, 64), 2.0, OP.is_ge)
        wrap(192, 256, A("GOOD"))
        yo, eo = 0, 0
        for c in range(4):
            w = 256 - 64 * c
            tt(A("Y", yo, yo + w), A("XL", 64 * c, 256), A("TRI", 0, w), OP.add)
            for m in range(4):
                k = 64 * m + 16 * c + 15
                sc = A("SC", k, k + 1) if m < 3 else A("LBF", 4 * t + c, 4 * t + c + 1)
                ts(A("E", eo, eo + w), A("Y", yo, yo + w), sc, OP.is_equal, A("SC", 207 + 16 * c, 208 + 16 * c), OP.mult)
                mm(A("L0", 64 * c, 256), A("BLK"), A("E", eo, eo + w), c == 0 and m == 0, c == 3 and m == 3)
                eo += w
            yo += w
        scan(A("S4"), A("SG4"), A("L0", 0, 256))
        tt(A("WIN"), A("GOOD"), A("S4", 3, 256, 4), OP.is_gt)
        wrap(256, 320, A("WIN"))
        tt(A("KD", 0, 12), A("KP", 0, 12), A("TR", 0, 12), OP.subtract)
        tt(A("KD", 12, 16), A("KPB", 4 * t, 4 * t + 4), A("TR", 12, 16), OP.subtract)
        for c in range(4):
            ts(A("KO", c, 16, 4), A("KD", c, 16, 4), A("SC", 271 + 16 * c, 272 + 16 * c), OP.mult)
        tt(A("KD"), A("KO"), A("TR"), OP.add)
        ts(A("OS"), A("KD"), 128.0, OP.mult)
        for m, (u, v, sel) in enumerate(((1, 3, A("FI", 0, 64)), (0, 2, l("ML")), (3, 1, A("FI", 64, 128)), (2, 0, l("MK")))):
            tt(A("DV", 64 * m, 64 * m + 64), X(u), X(v), OP.subtract)
            tt(A("DL", 64 * m, 64 * m + 64), A("DV", 64 * m, 64 * m + 64), sel, OP.mult)
        tt(A("NEW"), A("ROWS"), A("DL"), OP.add)
        cp(IND(r4, A("OS")), A("NEW"))
        for i, nm in enumerate(("ROWS", "NEW")):
            for a in range(4):
                mm(A("L1", 64 * i, 64 * i + 64), A("TA", 128 * a, 128 * a + 128), A(nm, 64 * a, 64 * a + 64), a == 0, a == 3)
        ts(A("SL"), A("L1", 0, 128), float(NW - 1), OP.min)
        cp(A("AL", 0, 12), A("SC", 15, 192, 16)); cp(A("AL", 12, 16), A("LBF", 4 * t, 4 * t + 4))

    def stress(n, i):
        win = A("P%d" % (n % NP)); sp, z = "FZ", 2048; bi = -2048.0 if WI and n == 0 else 0.0
        act(A("O16"), IND(win, A("AL")), AF.Identity, bias=bi)
        for h in range(2):
            lo, hi = 512 * h, 512 * h + 512
            act(A("E", lo, hi), IND(win, A("SL", 64 * i + 32 * h, 64 * i + 32 * h + 32)), AF.Identity, bias=bi)
            mm(A("L%d" % h), A("I1"), A("E", lo, hi), True, False)
            for s in range(16):
                a = 64 * (s % 4) + 32 * h
                mm(A("L%d" % h, s, 512, 16), A("IM"), A("O16", a, a + 32), False, s == 15)
            ts(A("E", 1024 + lo, 1024 + hi), A("L%d" % h), -2047.0, OP.max, 2047.0, OP.min)
            act(A("E", 2048 + lo, 2048 + hi), A("E", 1024 + lo, 1024 + hi), AF.Sign)
        for h in range(2):
            b = A("L%d" % h); lo, hi = 1024 + 512 * h, 1536 + 512 * h
            mm(b, A("I1"), A("E", lo, hi), True, False); mm(b, A("IK"), A("E", lo + 1024, hi + 1024), False, True)
            act(A(sp, lo, hi), b, AF.Square)
        scan(A(sp, 2048 - z, 3072 - z), A("SEG"), A(sp, 1024, 2048))
        return A(sp, 2063 - z, 3072 - z, 16)

    def vote(t, e3):
        tt(A("WO"), e3, A("E1"), OP.is_gt)
        mm(A("L0", 0, 64), A("BLK"), A("WO"), True, True)
        tt(A("KEEP"), A("L0", 0, 64), A("QR", 64 * t, 64 * t + 64), OP.is_lt)
        for m in range(4):
            tt(A("DV", 64 * m, 64 * m + 64), A("DL", 64 * m, 64 * m + 64), A("KEEP"), OP.mult)
        tt(IND(A("R4"), A("OS")), A("ROWS"), A("DV"), OP.add)

    copies(CHUNKS[0], 0, V)
    for t in range(RO):
        n = 3 * t
        lanes(t); relist("WB")
        sweep(n, "WA")
        if t == 0:
            send([lambda T: T.MW[:, 0:GH], lambda T: T.MS[:, 0:GH], lambda T: T.MS[:, GH:768]], "MW", "arrm", [A("MW", 0, GH), A("MS")], [arrived[1]])
        gcp(A("E1"), stress(n, 0))
        sweep(n + 1, "WB")
        vote(t, stress(n + 2, 1)); relist("WA")
        sweep(n + 2, "WB")

    c0 = 0
    for k, w in enumerate(CHUNKS[3][0]):
        features(9, "WA", CHUNKS[3], k)
        b = A("S%d" % (cnt["s"] % 3), 0, w); cnt["s"] += 1
        Z = lambda i, lo, hi: A("FZ", 2048 * i + lo, 2048 * i + hi)
        for p in range(4):
            u = A(("D0", "D1", "D2", "L0", "L1")[cnt["d"] % 5], 0, w); cnt["d"] += 1
            mm(u, A("I1"), A("C16", 4 * c0 + p * w, 4 * c0 + p * w + w), True, False)
            mm(u, A("IK"), A("S16", 4 * c0 + p * w, 4 * c0 + p * w + w), False, True)
            act(Z(k % 2, p * w, p * w + w), u, AF.Square)
        for h in range(2):
            act(Z(k % 2, 2 * h * w, 2 * h * w + 2 * w), Z(k % 2, 2 * h * w, 2 * h * w + 2 * w), AF.Exp, scale=-2.0 ** -19)
        for p in range(4):
            off = A("WA", 128 * p + c0 // 16, 128 * p + (c0 + w) // 16)
            tt(Z(2 + k % 2, p * w, p * w + w), IND(A("MW"), off), Z(k % 2, p * w, p * w + w), OP.mult)
            mm(b, A("IF"), Z(2 + k % 2, p * w, p * w + w), p == 0, p == 3)
        act(A("R4", c0, c0 + w), b, AF.Identity)
        dma([lambda T, c0=c0, w=w: (T.y[:, c0:c0 + w], T.R4[:, c0:c0 + w])], [A("R4", c0, c0 + w)], [])
        c0 += w
    return ops


def schedule(ops):
    n = len(ops); succ = [[] for _ in range(n)]
    for k, o in enumerate(ops):
        for d in o["deps"]: succ[d].append(k)
    lat = lambda d, k: 0.0 if ops[d]["eng"] == "p" and ops[k]["eng"] == "p" else ops[d]["lat"]
    pr = [0.0] * n
    for k in range(n - 1, -1, -1):
        pr[k] = ops[k]["cost"] + max([pr[s] + lat(k, s) for s in succ[k]] + [ops[k]["lat"]])
    pred = [o["deps"] for o in ops]

    def run(before, after, pr, fwd):
        left = [len(b) for b in before]; ready = [0.0 if fwd else o["lat"] for o in ops]; free = {}; pool = {}; order = []; at = [0.0] * n
        for k in range(n):
            if not left[k]: pool.setdefault(ops[k]["eng"], []).append(k)
        end = 0.0
        while len(order) < n:
            best = None
            for e, L in pool.items():
                if not L: continue
                t = max(free.get(e, 0.0), min(ready[k] for k in L))
                if best is None or t < best[0]: best = (t, e)
            t, e = best
            k = max((k for k in pool[e] if ready[k] <= t + WAIT), key=lambda k: (pr[k], -k))
            t = max(t, ready[k])
            pool[e].remove(k); order.append(k); fin = t + ops[k]["cost"]; at[k] = t
            if e != "x": free[e] = fin
            end = max(end, fin + (ops[k]["lat"] if fwd else 0.0))
            for s in after[k]:
                ready[s] = max(ready[s], fin + (lat(k, s) if fwd else lat(s, k))); left[s] -= 1
                if not left[s]: pool.setdefault(ops[s]["eng"], []).append(s)
        return order, end, at

    best = run(pred, succ, pr, True); cur = best
    for _ in range(PASSES):
        back = run(succ, pred, [cur[2][k] + ops[k]["cost"] for k in range(n)], False)
        cur = run(pred, succ, [back[2][k] + ops[k]["cost"] for k in range(n)], True)
        if cur[1] < best[1]: best = cur
    for k in range(n): ops[k]["t"] = best[2][k]
    return best[0], best[1]


def plan():
    ops = build(); order, end = schedule(ops)
    sems = {"v": "cv", "a": "ca", "p": "cp", "g": "cg"}
    count, known, done, steps, nd = {}, {}, {}, [], 0
    for k in order:
        o = ops[k]; e = o["eng"]
        if e == "x":
            done[k] = (o["fn"], -1, {}); count[o["fn"]] = -1
            continue
        kn = known.setdefault(e, {}); need = {}
        for d in o["deps"]:
            if e == "p" and ops[d]["eng"] == "p": continue
            s, v, _ = done[d]
            if s == "sent": v = count[s]
            if s not in need or need[s][0] < v: need[s] = (v, d)
        waits = []
        for s, (v, d) in sorted(need.items(), key=lambda it: -ops[it[1][1]]["t"]):
            if s in kn and kn[s] >= v: continue
            waits.append((s, v)); kn[s] = v
            for s2, v2 in done[d][2].items():
                if s2 not in kn or kn[s2] < v2: kn[s2] = v2
        if o.get("dma"):
            s = "dm%d" % nd; nd += 1; v = 16 * len(o["fn"])
        elif isinstance(o["fn"], tuple):
            s = "sent"; v = count.get(s, 0) + 1
        else:
            s = sems[e]; v = count.get(s, 0) + 1
        if s: count[s] = v
        done[k] = (s, v, dict(kn))
        steps.append((o, waits, s))
    return steps, count, end


PLAN = []


def masks(T, topo, r):
    N = len(T.cores); src = T.cores[r]; dst = [T.cores[(r + d) % N] for d in DS]
    far = [b for b in range(3) if topo.chip(dst[b]) != topo.chip(src)]; near = [b for b in range(3) if b not in far]
    ef = [e for e in topo.engines(src, dst[far[0]]) if all(e in topo.engines(src, dst[b]) for b in far)] if far else []
    out = {}
    for grp, eng in ((far, ef), (near, [e for e in topo.engines(src, dst[near[0]]) if e not in ef] if near else [])):
        if grp:
            k = 1
            while 2 * k * len(grp) <= len(eng): k *= 2
            for i, b in enumerate(grp): out[b] = eng[i * k:(i + 1) * k]
    return [out[b] for b in range(3)]


def rank_program(g, core, T, topo):
    r = T.rank_of(core)
    if r is None:
        return
    if not PLAN: PLAN.append(plan())
    steps, count, _ = PLAN[0]
    N = len(T.cores); mine = masks(T, topo, r)
    arrive = sum(len(masks(T, topo, (r - DS[b]) % N)[b]) for b in range(3))
    Q = {"v": g.vector, "a": g.scalar, "p": g.tensor, "g": g, "s": g.sync}
    val = lambda s, v: arrive if v < 0 else v * sum(len(m) for m in mine) if s == "sent" else v
    for o, waits, s in steps:
        q = Q[o["eng"]]
        for ws, wv in waits:
            q.wait_ge(T.sem[ws], val(ws, wv))
        if o.get("dma"):
            for f in o["fn"]:
                dst, src = f(T)
                (q.dma_start(dst, src, accum_op=OP.add) if o.get("acc") else q.dma_start(dst, src)).then_inc(T.sem[s], 16)
        elif isinstance(o["fn"], tuple):
            _, srcs, dst, sem = o["fn"]; trs = []
            for b in range(3):
                rid, pid, _ = topo.addr(T.cores[(r + DS[b]) % N])
                trs.append(RemoteDMATransfer(dst_ids=[DstId(rid=rid, pnc=pid)], dma_engine_mask=sum(1 << e for e in mine[b]), remote_sem=T.sem[sem],
                                             src=srcs[b](T), dst=T[dst][:, V + b * GH:V + (b + 1) * GH]))
            g.remote_dma_fused(trs, local_sem=T.sem.sent)
        else:
            o["fn"](g, T, r).then_inc(T.sem[s], 1)
    for s, v in count.items():
        g.wait_ge(T.sem[s], val(s, v))
